import numpy as np
import ml_dtypes


def mxq(x, axis, fmt="e4m3"):
    dtype, down = {"e4m3": (ml_dtypes.float8_e4m3fn, 7), "e5m2": (ml_dtypes.float8_e5m2, 14)}[fmt]
    v = np.moveaxis(np.asarray(x, np.float32).astype(ml_dtypes.bfloat16).astype(np.float64), axis, -1)
    blocks = v.reshape(v.shape[:-1] + (-1, 32))
    amax = np.abs(blocks).max(-1, keepdims=True)
    byte = np.maximum(np.where(amax > 0, np.frexp(amax)[1] - 1 + 127, 0) - down, 1)
    scale = np.exp2(byte - 127.0)
    codes = (blocks / scale).astype(np.float32).astype(dtype).astype(np.float64)
    return np.moveaxis((codes * scale).reshape(v.shape), -1, axis)


WIDE = False


def mx_kscale(k):
    if not WIDE:
        return np.ones(k)
    levels = np.array([10, -10, 5, -5, 0])
    if k % 512:
        return np.exp2(np.random.permutation(np.resize(levels, k // 32))).repeat(32)
    a = np.empty((k // 512, 16))
    for p in range(k // 512):
        a[p, :8] = np.random.permutation(np.resize(levels, 8))
        for g in range(8):
            far = levels[np.abs(levels - a[p, g]) >= 10]
            a[p, g + 8] = far[np.random.randint(len(far))]
    return np.exp2(a.ravel()).repeat(32)


def f64(x):
    return np.asarray(x).astype(np.float64)


def striped(idx):
    return np.tile(idx.reshape(-1, 16).T, (8, 1)).astype(np.uint16)


def unstriped(offs):
    return offs[:16].T.reshape(-1).astype(np.int64)


def pack_weight(w):
    k, n = w.shape
    w = f64(np.asarray(w, np.float32).astype(ml_dtypes.bfloat16)).reshape(k // 32, 32, n)
    amax = np.abs(w).max(1)
    byte = np.clip(np.where(amax > 0, np.frexp(amax)[1] - 1 + 127 - 7, 1), 1, 254)
    scaled = (w * np.exp2(127.0 - byte)[:, None, :]).reshape(k, n).astype(np.float32)
    words = np.ascontiguousarray(scaled.reshape(k // 512, 128, 4, n).transpose(0, 1, 3, 2)).astype(ml_dtypes.float8_e4m3fn).view(np.uint8)
    return words, np.ascontiguousarray(byte.astype(np.uint8).reshape(k // 512, 16, n))


def unpack_weight(words, scales):
    g, p, n, _ = words.shape
    vals = np.ascontiguousarray(words).view(ml_dtypes.float8_e4m3fn).astype(np.float64) * np.repeat(np.exp2(scales.astype(np.float64) - 127.0), 8, axis=1)[..., None]
    return vals.transpose(0, 1, 3, 2).reshape(g * 512, n)


K, T, S, N, U, D = 512, 1024, 512, 256, 256, 4
P = 2 ** 7


def setup_inputs():
    n = np.random.standard_normal
    s = mx_kscale(K)[:, None]
    packed_xT = pack_weight(n((K, T)) * s)
    return {
        "x_words": packed_xT[0],
        "x_scales": packed_xT[1],
        "w1": (n((K, N)) / np.sqrt(K) / s).astype(np.float32),
        "w2": (n((K, N)) / np.sqrt(K) / s).astype(np.float32),
        "w3": (n((K, N)) / np.sqrt(K) / s).astype(np.float32),
        "px": (n((N, U))).astype(np.float32),
        "py": (n((N, U))).astype(np.float32),
        "wgt": (np.tile(np.random.uniform(0.1, 0.6, (D, 1, U)), (1, P, 1))).astype(np.float32),
        "offs": striped(np.random.permutation(T)[:S]),
        "jt1": striped(np.random.randint(0, S, U)),
        "jt2": striped(np.random.randint(0, S, U)),
        "jt3": striped(np.random.randint(0, S, U)),
        "jt4": striped(np.random.randint(0, S, U)),
    }


def reference(x_words, x_scales, w1, w2, w3, px, py, wgt, offs, jt1, jt2, jt3, jt4):
    xq = unpack_weight(x_words, x_scales)[:, unstriped(offs)]
    ra = mxq(f64(w1), 0, "e4m3").T @ xq
    rb = mxq(f64(w2), 0, "e4m3").T @ xq
    tr = mxq(f64(w3), 0, "e4m3").T @ xq
    return f64(wgt)[0, :1] * (ra[:, unstriped(jt1)] * f64(px) - (rb[:, unstriped(jt1)] * f64(py)) + tr[:, unstriped(jt1)]) + f64(wgt)[1, :1] * (ra[:, unstriped(jt2)] * f64(px) - (rb[:, unstriped(jt2)] * f64(py)) + tr[:, unstriped(jt2)]) + f64(wgt)[2, :1] * (ra[:, unstriped(jt3)] * f64(px) - (rb[:, unstriped(jt3)] * f64(py)) + tr[:, unstriped(jt3)]) + f64(wgt)[3, :1] * (ra[:, unstriped(jt4)] * f64(px) - (rb[:, unstriped(jt4)] * f64(py)) + tr[:, unstriped(jt4)])

@@ -1,0 +1,172 @@
+from contextlib import ExitStack
+
+import concourse.mybir as mybir
+from concourse.masks import make_identity
+
+K, T, S, N, U, D = 512, 1024, 512, 256, 256, 4
+FLOPS = 3 * 2 * K * N * S
+
+F32 = mybir.dt.float32
+BF16 = mybir.dt.bfloat16
+I32 = mybir.dt.int32
+U32 = mybir.dt.uint32
+U16 = mybir.dt.uint16
+U8 = mybir.dt.uint8
+FP8X4 = mybir.dt.float8_e4m3fn_x4
+COPY = mybir.ActivationFunctionType.Copy
+MULT = mybir.AluOpType.mult
+ADD = mybir.AluOpType.add
+
+P = 128
+PACK = 4
+BLOCKS = N // P
+HALVES = U // P
+LAST = D - 1
+
+
+def tile_picked_yskinlb_lin_p_kernel(
+    tc, x_words, x_scales, w1, w2, w3, px, py, wgt, offs, jt1, jt2, jt3, jt4, out
+):
+    nc = tc.nc
+    with ExitStack() as ctx:
+        keep = ctx.enter_context(tc.tile_pool(name="keep", bufs=1))
+        ring = ctx.enter_context(tc.tile_pool(name="ring", bufs=4))
+        psum = ctx.enter_context(tc.psum_pool(name="psum", bufs=1))
+
+        order = [(blk, name) for blk in range(BLOCKS) for name in ("tr", "ra", "rb")]
+        weights = {"tr": w3, "ra": w1, "rb": w2}
+
+        def load_weight(blk, name):
+            raw = keep.tile([P, PACK, P], F32, name=f"raw_{name}{blk}")
+            nc.sync.dma_start(raw[:], weights[name].rearrange("(p j) n -> p j n", j=PACK)[:, :, blk * P : (blk + 1) * P])
+            return raw
+
+        def load_list(src, name):
+            tile = keep.tile(list(src.shape), U16, name=name)
+            nc.sync.dma_start(tile[:], src)
+            return tile
+
+        scale_table = keep.tile([P, T], U8, name="scale_table", align_bytes=64)
+        nc.vector.memset(scale_table[:].bitcast(I32), 0)
+        for q in range(4):
+            nc.scalar.dma_start(
+                scale_table[32 * q : 32 * q + 4, :].bitcast(I32), x_scales[0, 4 * q : 4 * q + 4, :].bitcast(I32)
+            )
+        picks = load_list(offs, "picks")
+        word_table = keep.tile([P, T], U32, name="word_table", align_bytes=64)
+        nc.sync.dma_start(word_table[:].bitcast(I32), x_words[0].rearrange("p n t -> p (n t)").bitcast(I32))
+        raws = {order[0]: load_weight(*order[0])}
+        joints = [load_list(src, f"joints{d}") for d, src in enumerate((jt1, jt2, jt3, jt4))]
+        raws[order[1]] = load_weight(*order[1])
+        rest = {}
+        rest["ra"] = keep.tile([P, BLOCKS, U], F32, name="rest_x")
+        nc.sync.dma_start(rest["ra"][:], px.rearrange("(b p) r -> p b r", p=P))
+        weight_rows = keep.tile([P, P], F32, name="weight_rows")
+        nc.gpsimd.memset(weight_rows[:], 0.0)
+        nc.sync.dma_start(weight_rows[0 : D * HALVES, :], wgt[:, 0, :].rearrange("d (h r) -> d h r", r=P))
+        raws[order[2]] = load_weight(*order[2])
+        rest["rb"] = keep.tile([P, BLOCKS, U], F32, name="rest_y")
+        nc.sync.dma_start(rest["rb"][:], py.rearrange("(b p) r -> p b r", p=P))
+        for key in order[3:]:
+            raws[key] = load_weight(*key)
+        last_weight = keep.tile([P, U], F32, name="last_weight")
+        nc.sync.dma_start(last_weight[:], wgt[LAST])
+
+        identity = keep.tile([P, P], F32, name="identity")
+        make_identity(nc, identity[:])
+
+        x_codes = keep.tile([P, S], U32, name="x_codes", align_bytes=64)
+        x_bytes = keep.tile([P, S], U8, name="x_bytes", align_bytes=64)
+
+        def quantise(key):
+            blk, name = key
+            grouped = keep.tile([P, P, PACK], BF16, name=f"grouped_{name}{blk}", align_bytes=64)
+            nc.scalar.copy(
+                grouped[:].rearrange("p (c i) t -> p c t i", i=4),
+                raws[key][:].rearrange("p t (c i) -> p c t i", i=4),
+            )
+            codes = keep.tile([P, P], U32, name=f"codes_{name}{blk}", align_bytes=64)
+            scales = keep.tile([P, P], U8, name=f"scales_{name}{blk}", align_bytes=64)
+            nc.vector.quantize_mx(
+                out=codes[:].bitcast(FP8X4), scales=scales[:], in_=grouped[:].rearrange("p c t -> p (c t)")
+            )
+            return codes, scales
+
+        def multiply(key, quantised, window, cols):
+            codes, scales = quantised
+            bank = psum.tile([P, cols.stop - cols.start], F32, name="product", bufs=2)
+            nc.tensor.matmul_mx(
+                out=bank[:],
+                lhsT=codes[:].bitcast(FP8X4),
+                lhsT_scale=scales[:],
+                rhs=x_codes[:, cols].bitcast(FP8X4),
+                rhs_scale=x_bytes[:, cols],
+                start=True,
+                stop=True,
+            )
+            nc.scalar.activation(window[:, cols], bank[:], COPY, scale=-1.0 if key[1] == "rb" else 1.0)
+
+        windows = {key: keep.tile([P, S], F32, name=f"window_{key[1]}{key[0]}") for key in order}
+
+        nc.vector.tensor_copy(x_bytes[:], scale_table[:].indirect(picks[:]))
+        quantised = {order[0]: quantise(order[0])}
+        for half in range(2):
+            cols = slice(half * S // 2, (half + 1) * S // 2)
+            nc.vector.tensor_copy(
+                x_codes[:, cols], word_table[:].indirect(picks[:, cols.start // 16 : cols.stop // 16])
+            )
+            multiply(order[0], quantised[order[0]], windows[order[0]], cols)
+        quantised[order[1]] = quantise(order[1])
+        multiply(order[1], quantised[order[1]], windows[order[1]], slice(0, S))
+
+        turned_weights = psum.tile([P, P], F32, name="product", bufs=2)
+        nc.tensor.transpose(turned_weights[:], weight_rows[:], identity[:])
+        weight_cols = keep.tile([P, D * HALVES], F32, name="weight_cols")
+        nc.scalar.copy(weight_cols[:], turned_weights[:, 0 : D * HALVES])
+
+        totals = [psum.tile([P, U], F32, name=f"total{blk}") for blk in range(BLOCKS)]
+        sums = {}
+
+        def turn(dst, src, first, last):
+            for h in range(HALVES):
+                nc.tensor.matmul(
+                    dst(h), src(h), identity[:], start=first and h == 0, stop=last and h == HALVES - 1, is_transpose=True
+                )
+
+        for step, key in enumerate(order):
+            blk, name = key
+            if step + 2 < len(order):
+                ahead = order[step + 2]
+                quantised[ahead] = quantise(ahead)
+                multiply(ahead, quantised[ahead], windows[ahead], slice(0, S))
+            for d in range(D):
+                if name == "tr" and d == LAST:
+                    continue
+                term = ring.tile([P, U], F32, name="term")
+                looked_up = windows[key][:].indirect(joints[d][:])
+                if name == "tr":
+                    nc.vector.tensor_copy(term[:], looked_up)
+                else:
+                    nc.vector.tensor_tensor(term[:], looked_up, rest[name][:, blk, :], MULT)
+                first = (blk, d) not in sums
+                if first:
+                    sums[blk, d] = psum.tile([P, HALVES, P], F32, name="joint_sum", bufs=4)
+                turn(lambda h: sums[blk, d][:, h, :], lambda h: term[:, h * P : (h + 1) * P], first, name == "rb")
+                if name == "rb":
+                    scaled = ring.tile([P, HALVES, P], F32, name="scaled")
+                    for h in range(HALVES):
+                        col = d * HALVES + h
+                        nc.scalar.activation(
+                            scaled[:, h, :], sums[blk, d][:, h, :], COPY, scale=weight_cols[:, col : col + 1]
+                        )
+                    turn(lambda h: totals[blk][:, h * P : (h + 1) * P], lambda h: scaled[:, h, :], d == 0, d == LAST)
+
+        direct = []
+        for blk in range(BLOCKS):
+            term = ring.tile([P, U], F32, name="term")
+            nc.vector.tensor_tensor(term[:], windows[blk, "tr"][:].indirect(joints[LAST][:]), last_weight[:], MULT)
+            direct.append(term)
+        for blk in range(BLOCKS):
+            result = keep.tile([P, U], F32, name=f"result{blk}")
+            nc.vector.tensor_tensor(result[:], totals[blk][:], direct[blk][:], ADD)
+            nc.sync.dma_start(out[blk * P : (blk + 1) * P, :], result[:])

@@ -21,7 +21,9 @@ P = 128
 PACK = 4
 BLOCKS = N // P
 HALVES = U // P
-LAST = D - 1
+PIECES = (slice(0, S // 2), slice(S // 2, S))
+DIRECT = ((1, 2), (1, 3), (0, 3))
+FIRST_DIRECT = min(d for blk, d in DIRECT)
 
 
 def tile_picked_yskinlb_lin_p_kernel(
@@ -33,12 +35,9 @@ def tile_picked_yskinlb_lin_p_kernel(
         ring = ctx.enter_context(tc.tile_pool(name="ring", bufs=4))
         psum = ctx.enter_context(tc.psum_pool(name="psum", bufs=1))
 
-        order = [(blk, name) for blk in range(BLOCKS) for name in ("tr", "ra", "rb")]
-        weights = {"tr": w3, "ra": w1, "rb": w2}
-
-        def load_weight(blk, name):
-            raw = keep.tile([P, PACK, P], F32, name=f"raw_{name}{blk}")
-            nc.sync.dma_start(raw[:], weights[name].rearrange("(p j) n -> p j n", j=PACK)[:, :, blk * P : (blk + 1) * P])
+        def load_weight(src, cols, tag):
+            raw = keep.tile([P, PACK, cols.stop - cols.start], F32, name=f"raw_{tag}", tag=tag, align_bytes=64)
+            nc.sync.dma_start(raw[:], src.rearrange("(p j) n -> p j n", j=PACK)[:, :, cols])
             return raw
 
         def load_list(src, name):
@@ -46,44 +45,57 @@ def tile_picked_yskinlb_lin_p_kernel(
             nc.sync.dma_start(tile[:], src)
             return tile
 
+        def load_rest(src, name):
+            tile = keep.tile([P, BLOCKS, U], F32, name=name)
+            nc.sync.dma_start(tile[:], src.rearrange("(b p) r -> p b r", p=P))
+            return tile
+
         scale_table = keep.tile([P, T], U8, name="scale_table", align_bytes=64)
-        nc.vector.memset(scale_table[:].bitcast(I32), 0)
-        for q in range(4):
-            nc.scalar.dma_start(
-                scale_table[32 * q : 32 * q + 4, :].bitcast(I32), x_scales[0, 4 * q : 4 * q + 4, :].bitcast(I32)
-            )
+        nc.gpsimd.memset(scale_table[:].bitcast(I32), 0)
         picks = load_list(offs, "picks")
         word_table = keep.tile([P, T], U32, name="word_table", align_bytes=64)
         nc.sync.dma_start(word_table[:].bitcast(I32), x_words[0].rearrange("p n t -> p (n t)").bitcast(I32))
-        raws = {order[0]: load_weight(*order[0])}
-        joints = [load_list(src, f"joints{d}") for d, src in enumerate((jt1, jt2, jt3, jt4))]
-        raws[order[1]] = load_weight(*order[1])
-        rest = {}
-        rest["ra"] = keep.tile([P, BLOCKS, U], F32, name="rest_x")
-        nc.sync.dma_start(rest["ra"][:], px.rearrange("(b p) r -> p b r", p=P))
+        for q in range(4):
+            nc.sync.dma_start(
+                scale_table[32 * q : 32 * q + 4, :].bitcast(I32), x_scales[0, 4 * q : 4 * q + 4, :].bitcast(I32)
+            )
+        raw_w3_0 = load_weight(w3, slice(0, P), "w3_0")
+        raw_w1 = load_weight(w1, slice(0, N), "w1")
+        joints = [load_list(jt1, "joints0")]
+        raw_w2 = load_weight(w2, slice(0, N), "w2")
+        joints.append(load_list(jt2, "joints1"))
+        joints.append(load_list(jt3, "joints2"))
+        rest = {"ra": load_rest(px, "rest_x")}
+        joints.append(load_list(jt4, "joints3"))
+        raw_w3_1 = load_weight(w3, slice(P, N), "w3_1")
         weight_rows = keep.tile([P, P], F32, name="weight_rows")
         nc.gpsimd.memset(weight_rows[:], 0.0)
         nc.sync.dma_start(weight_rows[0 : D * HALVES, :], wgt[:, 0, :].rearrange("d (h r) -> d h r", r=P))
-        raws[order[2]] = load_weight(*order[2])
-        rest["rb"] = keep.tile([P, BLOCKS, U], F32, name="rest_y")
-        nc.sync.dma_start(rest["rb"][:], py.rearrange("(b p) r -> p b r", p=P))
-        for key in order[3:]:
-            raws[key] = load_weight(*key)
-        last_weight = keep.tile([P, U], F32, name="last_weight")
-        nc.sync.dma_start(last_weight[:], wgt[LAST])
+        rest["rb"] = load_rest(py, "rest_y")
+        spread = keep.tile([P, D - FIRST_DIRECT, U], F32, name="spread")
+        nc.sync.dma_start(spread[:], wgt[FIRST_DIRECT:D].rearrange("d p r -> p d r"))
+        raws = {
+            (0, "tr"): raw_w3_0[:],
+            (1, "tr"): raw_w3_1[:],
+            (0, "ra"): raw_w1[:, :, 0:P],
+            (1, "ra"): raw_w1[:, :, P:N],
+            (0, "rb"): raw_w2[:, :, 0:P],
+            (1, "rb"): raw_w2[:, :, P:N],
+        }
 
         identity = keep.tile([P, P], F32, name="identity")
         make_identity(nc, identity[:])
 
         x_codes = keep.tile([P, S], U32, name="x_codes", align_bytes=64)
-        x_bytes = keep.tile([P, S], U8, name="x_bytes", align_bytes=64)
+        x_bytes = []
+        windows = {key: keep.tile([P, S], F32, name=f"window_{key[1]}{key[0]}") for key in raws}
 
         def quantise(key):
             blk, name = key
             grouped = keep.tile([P, P, PACK], BF16, name=f"grouped_{name}{blk}", align_bytes=64)
             nc.scalar.copy(
                 grouped[:].rearrange("p (c i) t -> p c t i", i=4),
-                raws[key][:].rearrange("p t (c i) -> p c t i", i=4),
+                raws[key].rearrange("p t (c i) -> p c t i", i=4),
             )
             codes = keep.tile([P, P], U32, name=f"codes_{name}{blk}", align_bytes=64)
             scales = keep.tile([P, P], U8, name=f"scales_{name}{blk}", align_bytes=64)
@@ -92,40 +104,43 @@ def tile_picked_yskinlb_lin_p_kernel(
             )
             return codes, scales
 
-        def multiply(key, quantised, window, cols):
+        def multiply(quantised, pieces):
             codes, scales = quantised
-            bank = psum.tile([P, cols.stop - cols.start], F32, name="product", bufs=2)
-            nc.tensor.matmul_mx(
-                out=bank[:],
-                lhsT=codes[:].bitcast(FP8X4),
-                lhsT_scale=scales[:],
-                rhs=x_codes[:, cols].bitcast(FP8X4),
-                rhs_scale=x_bytes[:, cols],
-                start=True,
-                stop=True,
-            )
-            nc.scalar.activation(window[:, cols], bank[:], COPY, scale=-1.0 if key[1] == "rb" else 1.0)
+            bank = psum.tile([P, S], F32, name="product", bufs=2)
+            for piece in pieces:
+                cols = PIECES[piece]
+                nc.tensor.matmul_mx(
+                    out=bank[:, cols],
+                    lhsT=codes[:].bitcast(FP8X4),
+                    lhsT_scale=scales[:],
+                    rhs=x_codes[:, cols].bitcast(FP8X4),
+                    rhs_scale=x_bytes[piece][:],
+                    start=True,
+                    stop=True,
+                )
+            return bank
 
-        windows = {key: keep.tile([P, S], F32, name=f"window_{key[1]}{key[0]}") for key in order}
+        def make_window(key):
+            bank = multiply(quantise(key), (0, 1))
+            nc.scalar.activation(windows[key][:], bank[:], COPY, scale=-1.0 if key[1] == "rb" else 1.0)
 
-        nc.vector.tensor_copy(x_bytes[:], scale_table[:].indirect(picks[:]))
-        quantised = {order[0]: quantise(order[0])}
-        for half in range(2):
-            cols = slice(half * S // 2, (half + 1) * S // 2)
+        nc.vector.tensor_copy(x_codes[:], word_table[:].indirect(picks[:]))
+        first_weight = quantise((0, "tr"))
+        banks = []
+        for piece, cols in enumerate(PIECES):
+            x_bytes.append(keep.tile([P, S // 2], U8, name=f"x_bytes{piece}", tag=("bytes0", "w3_0")[piece], align_bytes=64))
             nc.vector.tensor_copy(
-                x_codes[:, cols], word_table[:].indirect(picks[:, cols.start // 16 : cols.stop // 16])
+                x_bytes[piece][:], scale_table[:].indirect(picks[:, cols.start // 16 : cols.stop // 16])
             )
-            multiply(order[0], quantised[order[0]], windows[order[0]], cols)
-        quantised[order[1]] = quantise(order[1])
-        multiply(order[1], quantised[order[1]], windows[order[1]], slice(0, S))
-
-        turned_weights = psum.tile([P, P], F32, name="product", bufs=2)
-        nc.tensor.transpose(turned_weights[:], weight_rows[:], identity[:])
-        weight_cols = keep.tile([P, D * HALVES], F32, name="weight_cols")
-        nc.scalar.copy(weight_cols[:], turned_weights[:, 0 : D * HALVES])
+            banks.append(multiply(first_weight, (piece,)))
+        for piece, cols in enumerate(PIECES):
+            nc.vector.tensor_copy(windows[0, "tr"][:, cols], banks[piece][:, cols])
+        make_window((0, "ra"))
+        make_window((1, "ra"))
 
         totals = [psum.tile([P, U], F32, name=f"total{blk}") for blk in range(BLOCKS)]
         sums = {}
+        weight_cols = keep.tile([P, D * HALVES], F32, name="weight_cols")
 
         def turn(dst, src, first, last):
             for h in range(HALVES):
@@ -133,21 +148,16 @@ def tile_picked_yskinlb_lin_p_kernel(
                     dst(h), src(h), identity[:], start=first and h == 0, stop=last and h == HALVES - 1, is_transpose=True
                 )
 
-        for step, key in enumerate(order):
-            blk, name = key
-            if step + 2 < len(order):
-                ahead = order[step + 2]
-                quantised[ahead] = quantise(ahead)
-                multiply(ahead, quantised[ahead], windows[ahead], slice(0, S))
-            for d in range(D):
-                if name == "tr" and d == LAST:
-                    continue
-                term = ring.tile([P, U], F32, name="term")
-                looked_up = windows[key][:].indirect(joints[d][:])
+        def gather_step(blk, items, tag):
+            items = [(name, d) for name, d in items if not (name == "tr" and (blk, d) in DIRECT)]
+            terms = keep.tile([P, len(items), U], F32, name=f"terms_{tag}", tag=tag, align_bytes=64)
+            for i, (name, d) in enumerate(items):
+                term = terms[:, i, :]
+                looked_up = windows[blk, name][:].indirect(joints[d][:])
                 if name == "tr":
-                    nc.vector.tensor_copy(term[:], looked_up)
+                    nc.vector.tensor_copy(term, looked_up)
                 else:
-                    nc.vector.tensor_tensor(term[:], looked_up, rest[name][:, blk, :], MULT)
+                    nc.vector.tensor_tensor(term, looked_up, rest[name][:, blk, :], MULT)
                 first = (blk, d) not in sums
                 if first:
                     sums[blk, d] = psum.tile([P, HALVES, P], F32, name="joint_sum", bufs=4)
@@ -159,14 +169,29 @@ def tile_picked_yskinlb_lin_p_kernel(
                         nc.scalar.activation(
                             scaled[:, h, :], sums[blk, d][:, h, :], COPY, scale=weight_cols[:, col : col + 1]
                         )
-                    turn(lambda h: totals[blk][:, h * P : (h + 1) * P], lambda h: scaled[:, h, :], d == 0, d == LAST)
+                    turn(lambda h: totals[blk][:, h * P : (h + 1) * P], lambda h: scaled[:, h, :], d == 0, d == D - 1)
 
-        direct = []
-        for blk in range(BLOCKS):
-            term = ring.tile([P, U], F32, name="term")
-            nc.vector.tensor_tensor(term[:], windows[blk, "tr"][:].indirect(joints[LAST][:]), last_weight[:], MULT)
-            direct.append(term)
-        for blk in range(BLOCKS):
+        gather_step(0, [("tr", d) for d in range(D)], "w1")
+        make_window((0, "rb"))
+        make_window((1, "rb"))
+        gather_step(0, [("ra", d) for d in range(D)], "w2")
+        make_window((1, "tr"))
+        turned_weights = psum.tile([P, P], F32, name="product", bufs=2)
+        nc.tensor.transpose(turned_weights[:], weight_rows[:], identity[:])
+        nc.scalar.copy(weight_cols[:], turned_weights[:, 0 : D * HALVES])
+        gather_step(0, [("rb", d) for d in range(D)], "w3_1")
+        for d in range(D):
+            gather_step(1, [(name, d) for name in ("tr", "ra", "rb")], f"joint{d}")
+
+        direct = keep.tile([P, len(DIRECT), U], F32, name="direct", tag="joint1", align_bytes=64)
+        for i, (blk, d) in enumerate(DIRECT):
+            nc.vector.tensor_tensor(
+                direct[:, i, :], windows[blk, "tr"][:].indirect(joints[d][:]), spread[:, d - FIRST_DIRECT, :], MULT
+            )
+
+        pair = keep.tile([P, U], F32, name="pair")
+        nc.vector.tensor_tensor(pair[:], direct[:, 0, :], direct[:, 1, :], ADD)
+        for blk, extra in ((0, direct[:, 2, :]), (1, pair[:])):
             result = keep.tile([P, U], F32, name=f"result{blk}")
-            nc.vector.tensor_tensor(result[:], totals[blk][:], direct[blk][:], ADD)
+            nc.vector.tensor_tensor(result[:], totals[blk][:], extra, ADD)
             nc.sync.dma_start(out[blk * P : (blk + 1) * P, :], result[:])

@@ -19,11 +19,18 @@ ADD = mybir.AluOpType.add
 
 P = 128
 PACK = 4
+QUADRANT = 32
+LIST_ROWS = 16
+LINE = 4
 BLOCKS = N // P
 HALVES = U // P
-PIECES = (slice(0, S // 2), slice(S // 2, S))
-DIRECT = ((1, 2), (1, 3), (0, 3))
-FIRST_DIRECT = min(d for blk, d in DIRECT)
+MX_ALIGN = 64
+
+HALF = S // 2
+PIECES = ((0, 0, HALF), (1, 0, HALF // 2), (1, HALF // 2, HALF))
+
+LATE_TERMS = ((1, 2), (1, 3), (0, 3))
+FIRST_LATE_JOINT = min(d for blk, d in LATE_TERMS)
 
 
 def tile_picked_yskinlb_lin_p_kernel(
@@ -32,13 +39,25 @@ def tile_picked_yskinlb_lin_p_kernel(
     nc = tc.nc
     with ExitStack() as ctx:
         keep = ctx.enter_context(tc.tile_pool(name="keep", bufs=1))
-        ring = ctx.enter_context(tc.tile_pool(name="ring", bufs=4))
         psum = ctx.enter_context(tc.psum_pool(name="psum", bufs=1))
 
-        def load_weight(src, cols, tag):
-            raw = keep.tile([P, PACK, cols.stop - cols.start], F32, name=f"raw_{tag}", tag=tag, align_bytes=64)
-            nc.sync.dma_start(raw[:], src.rearrange("(p j) n -> p j n", j=PACK)[:, :, cols])
-            return raw
+        def product_bank(shape):
+            return psum.tile(shape, F32, name="product", bufs=2)
+
+        def joint_bank(shape):
+            return psum.tile(shape, F32, name="joint_sum", bufs=D)
+
+        staged = [[(0, "tr")], [(0, "ra")], [(0, "rb")], [(1, "tr"), (1, "ra")], [(1, "rb")]]
+        raw = {}
+        for i, keys in enumerate(staged):
+            stage = keep.tile([P, len(keys), PACK, P], F32, name=f"raw{i}", tag=f"stage{i}", align_bytes=MX_ALIGN)
+            for slot, key in enumerate(keys):
+                raw[key] = stage[:, slot]
+        weights = {"ra": w1, "rb": w2, "tr": w3}
+
+        def load_weight(blk, name):
+            rows = weights[name].rearrange("(p t) m -> p t m", t=PACK)
+            nc.sync.dma_start(raw[blk, name], rows[:, :, blk * P : (blk + 1) * P])
 
         def load_list(src, name):
             tile = keep.tile(list(src.shape), U16, name=name)
@@ -50,148 +69,148 @@ def tile_picked_yskinlb_lin_p_kernel(
             nc.sync.dma_start(tile[:], src.rearrange("(b p) r -> p b r", p=P))
             return tile
 
-        scale_table = keep.tile([P, T], U8, name="scale_table", align_bytes=64)
+        scale_table = keep.tile([P, T], U8, name="scale_table", align_bytes=MX_ALIGN)
         nc.gpsimd.memset(scale_table[:].bitcast(I32), 0)
         picks = load_list(offs, "picks")
-        word_table = keep.tile([P, T], U32, name="word_table", align_bytes=64)
-        nc.sync.dma_start(word_table[:].bitcast(I32), x_words[0].rearrange("p n t -> p (n t)").bitcast(I32))
-        for q in range(4):
+        load_weight(0, "tr")
+        for q in range(P // QUADRANT):
             nc.sync.dma_start(
-                scale_table[32 * q : 32 * q + 4, :].bitcast(I32), x_scales[0, 4 * q : 4 * q + 4, :].bitcast(I32)
+                scale_table[QUADRANT * q : QUADRANT * q + 4, :].bitcast(I32),
+                x_scales[0, 4 * q : 4 * q + 4, :].bitcast(I32),
             )
-        raw_w3_0 = load_weight(w3, slice(0, P), "w3_0")
-        raw_w1 = load_weight(w1, slice(0, N), "w1")
+        word_table = keep.tile([P, T], U32, name="word_table", align_bytes=MX_ALIGN)
+        nc.sync.dma_start(word_table[:].bitcast(I32), x_words[0].rearrange("p n t -> p (n t)").bitcast(I32))
+        load_weight(0, "ra")
         joints = [load_list(jt1, "joints0")]
-        raw_w2 = load_weight(w2, slice(0, N), "w2")
+        load_weight(0, "rb")
         joints.append(load_list(jt2, "joints1"))
         joints.append(load_list(jt3, "joints2"))
         rest = {"ra": load_rest(px, "rest_x")}
         joints.append(load_list(jt4, "joints3"))
-        raw_w3_1 = load_weight(w3, slice(P, N), "w3_1")
+        load_weight(1, "tr")
         weight_rows = keep.tile([P, P], F32, name="weight_rows")
         nc.gpsimd.memset(weight_rows[:], 0.0)
         nc.sync.dma_start(weight_rows[0 : D * HALVES, :], wgt[:, 0, :].rearrange("d (h r) -> d h r", r=P))
+        load_weight(1, "ra")
         rest["rb"] = load_rest(py, "rest_y")
-        spread = keep.tile([P, D - FIRST_DIRECT, U], F32, name="spread")
-        nc.sync.dma_start(spread[:], wgt[FIRST_DIRECT:D].rearrange("d p r -> p d r"))
-        raws = {
-            (0, "tr"): raw_w3_0[:],
-            (1, "tr"): raw_w3_1[:],
-            (0, "ra"): raw_w1[:, :, 0:P],
-            (1, "ra"): raw_w1[:, :, P:N],
-            (0, "rb"): raw_w2[:, :, 0:P],
-            (1, "rb"): raw_w2[:, :, P:N],
-        }
+        load_weight(1, "rb")
+        late_weights = keep.tile([P, D - FIRST_LATE_JOINT, U], F32, name="late_weights")
+        nc.sync.dma_start(late_weights[:], wgt[FIRST_LATE_JOINT:D].rearrange("d p r -> p d r"))
 
         identity = keep.tile([P, P], F32, name="identity")
         make_identity(nc, identity[:])
 
-        x_codes = keep.tile([P, S], U32, name="x_codes", align_bytes=64)
-        x_bytes = []
-        windows = {key: keep.tile([P, S], F32, name=f"window_{key[1]}{key[0]}") for key in raws}
+        windows = {key: keep.tile([P, S], F32, name=f"window_{key[1]}{key[0]}") for key in raw}
 
         def quantise(key):
             blk, name = key
-            grouped = keep.tile([P, P, PACK], BF16, name=f"grouped_{name}{blk}", align_bytes=64)
+            grouped = keep.tile([P, P, PACK], BF16, name=f"grouped_{name}{blk}", align_bytes=MX_ALIGN)
             nc.scalar.copy(
-                grouped[:].rearrange("p (c i) t -> p c t i", i=4),
-                raws[key].rearrange("p t (c i) -> p c t i", i=4),
+                grouped[:].rearrange("p (c i) t -> p c t i", i=LINE),
+                raw[key].rearrange("p t (c i) -> p c t i", i=LINE),
             )
-            codes = keep.tile([P, P], U32, name=f"codes_{name}{blk}", align_bytes=64)
-            scales = keep.tile([P, P], U8, name=f"scales_{name}{blk}", align_bytes=64)
+            codes = keep.tile([P, P], U32, name=f"codes_{name}{blk}", align_bytes=MX_ALIGN)
+            scales = keep.tile([P, P], U8, name=f"scales_{name}{blk}", align_bytes=MX_ALIGN)
             nc.vector.quantize_mx(
                 out=codes[:].bitcast(FP8X4), scales=scales[:], in_=grouped[:].rearrange("p c t -> p (c t)")
             )
             return codes, scales
 
-        def multiply(quantised, pieces):
+        def multiply(dst, quantised, half, lo, hi):
             codes, scales = quantised
-            bank = psum.tile([P, S], F32, name="product", bufs=2)
-            for piece in pieces:
-                cols = PIECES[piece]
-                nc.tensor.matmul_mx(
-                    out=bank[:, cols],
-                    lhsT=codes[:].bitcast(FP8X4),
-                    lhsT_scale=scales[:],
-                    rhs=x_codes[:, cols].bitcast(FP8X4),
-                    rhs_scale=x_bytes[piece][:],
-                    start=True,
-                    stop=True,
-                )
-            return bank
+            nc.tensor.matmul_mx(
+                out=dst,
+                lhsT=codes[:].bitcast(FP8X4),
+                lhsT_scale=scales[:],
+                rhs=picked_words[half][:, lo:hi].bitcast(FP8X4),
+                rhs_scale=picked_scales[:, half * HALF + lo : half * HALF + hi],
+                start=True,
+                stop=True,
+            )
 
         def make_window(key):
-            bank = multiply(quantise(key), (0, 1))
+            quantised = quantise(key)
+            bank = product_bank([P, S])
+            for half in range(2):
+                multiply(bank[:, half * HALF : (half + 1) * HALF], quantised, half, 0, HALF)
             nc.scalar.activation(windows[key][:], bank[:], COPY, scale=-1.0 if key[1] == "rb" else 1.0)
 
-        nc.vector.tensor_copy(x_codes[:], word_table[:].indirect(picks[:]))
+        picked_scales = keep.tile([P, S], U8, name="picked_scales", align_bytes=MX_ALIGN)
+        nc.vector.tensor_copy(picked_scales[:], scale_table[:].indirect(picks[:]))
         first_weight = quantise((0, "tr"))
-        banks = []
-        for piece, cols in enumerate(PIECES):
-            x_bytes.append(keep.tile([P, S // 2], U8, name=f"x_bytes{piece}", tag=("bytes0", "w3_0")[piece], align_bytes=64))
-            nc.vector.tensor_copy(
-                x_bytes[piece][:], scale_table[:].indirect(picks[:, cols.start // 16 : cols.stop // 16])
-            )
-            banks.append(multiply(first_weight, (piece,)))
-        for piece, cols in enumerate(PIECES):
-            nc.vector.tensor_copy(windows[0, "tr"][:, cols], banks[piece][:, cols])
+        picked_words = [
+            keep.tile([P, HALF], U32, name=f"picked_words{half}", tag=tag, align_bytes=MX_ALIGN)
+            for half, tag in enumerate(("picked_words", "stage0"))
+        ]
+        piece_banks = []
+        for half, lo, hi in PIECES:
+            entries = slice((half * HALF + lo) // LIST_ROWS, (half * HALF + hi) // LIST_ROWS)
+            nc.vector.tensor_copy(picked_words[half][:, lo:hi], word_table[:].indirect(picks[:, entries]))
+            piece_banks.append(joint_bank([P, hi - lo]))
+            multiply(piece_banks[-1][:], first_weight, half, lo, hi)
+        for (half, lo, hi), bank in zip(PIECES, piece_banks):
+            nc.vector.tensor_copy(windows[0, "tr"][:, half * HALF + lo : half * HALF + hi], bank[:])
         make_window((0, "ra"))
-        make_window((1, "ra"))
 
-        totals = [psum.tile([P, U], F32, name=f"total{blk}") for blk in range(BLOCKS)]
-        sums = {}
+        totals = [psum.tile([P, HALVES, P], F32, name=f"total{blk}") for blk in range(BLOCKS)]
+        joint_sums = {}
         weight_cols = keep.tile([P, D * HALVES], F32, name="weight_cols")
 
-        def turn(dst, src, first, last):
+        def add_transposed(bank, src, first, last):
             for h in range(HALVES):
                 nc.tensor.matmul(
-                    dst(h), src(h), identity[:], start=first and h == 0, stop=last and h == HALVES - 1, is_transpose=True
+                    bank[:, h, :],
+                    src[:, h, :],
+                    identity[:],
+                    start=first and h == 0,
+                    stop=last and h == HALVES - 1,
+                    is_transpose=True,
                 )
 
-        def gather_step(blk, items, tag):
-            items = [(name, d) for name, d in items if not (name == "tr" and (blk, d) in DIRECT)]
-            terms = keep.tile([P, len(items), U], F32, name=f"terms_{tag}", tag=tag, align_bytes=64)
+        def look_up(blk, items, tag):
+            items = [(name, d) for name, d in items if name != "tr" or (blk, d) not in LATE_TERMS]
+            terms = keep.tile([P, len(items), U], F32, name=f"terms_{tag}", tag=tag, align_bytes=MX_ALIGN)
             for i, (name, d) in enumerate(items):
-                term = terms[:, i, :]
                 looked_up = windows[blk, name][:].indirect(joints[d][:])
                 if name == "tr":
-                    nc.vector.tensor_copy(term, looked_up)
+                    nc.vector.tensor_copy(terms[:, i, :], looked_up)
                 else:
-                    nc.vector.tensor_tensor(term, looked_up, rest[name][:, blk, :], MULT)
-                first = (blk, d) not in sums
-                if first:
-                    sums[blk, d] = psum.tile([P, HALVES, P], F32, name="joint_sum", bufs=4)
-                turn(lambda h: sums[blk, d][:, h, :], lambda h: term[:, h * P : (h + 1) * P], first, name == "rb")
+                    nc.vector.tensor_tensor(terms[:, i, :], looked_up, rest[name][:, blk, :], MULT)
+                opens = (blk, d) not in joint_sums
+                if opens:
+                    joint_sums[blk, d] = joint_bank([P, HALVES, P])
+                halves = terms[:, i, :].rearrange("p (h r) -> p h r", h=HALVES)
+                add_transposed(joint_sums[blk, d], halves, opens, name == "rb")
                 if name == "rb":
-                    scaled = ring.tile([P, HALVES, P], F32, name="scaled")
+                    weighted = keep.tile([P, HALVES, P], F32, name="weighted", bufs=D)
                     for h in range(HALVES):
-                        col = d * HALVES + h
+                        col = HALVES * d + h
                         nc.scalar.activation(
-                            scaled[:, h, :], sums[blk, d][:, h, :], COPY, scale=weight_cols[:, col : col + 1]
+                            weighted[:, h, :], joint_sums[blk, d][:, h, :], COPY, scale=weight_cols[:, col : col + 1]
                         )
-                    turn(lambda h: totals[blk][:, h * P : (h + 1) * P], lambda h: scaled[:, h, :], d == 0, d == D - 1)
+                    add_transposed(totals[blk], weighted, d == 0, d == D - 1)
 
-        gather_step(0, [("tr", d) for d in range(D)], "w1")
+        look_up(0, [("tr", d) for d in range(D)], "stage1")
         make_window((0, "rb"))
-        make_window((1, "rb"))
-        gather_step(0, [("ra", d) for d in range(D)], "w2")
+        look_up(0, [("ra", d) for d in range(D)], "stage2")
         make_window((1, "tr"))
-        turned_weights = psum.tile([P, P], F32, name="product", bufs=2)
+        turned_weights = product_bank([P, P])
         nc.tensor.transpose(turned_weights[:], weight_rows[:], identity[:])
         nc.scalar.copy(weight_cols[:], turned_weights[:, 0 : D * HALVES])
-        gather_step(0, [("rb", d) for d in range(D)], "w3_1")
+        make_window((1, "ra"))
+        look_up(0, [("rb", d) for d in range(D)], "stage3")
+        make_window((1, "rb"))
+        look_up(1, [("tr", d) for d in range(D)], "stage4")
         for d in range(D):
-            gather_step(1, [(name, d) for name in ("tr", "ra", "rb")], f"joint{d}")
+            look_up(1, [("ra", d), ("rb", d)], f"joint{d}")
 
-        direct = keep.tile([P, len(DIRECT), U], F32, name="direct", tag="joint1", align_bytes=64)
-        for i, (blk, d) in enumerate(DIRECT):
-            nc.vector.tensor_tensor(
-                direct[:, i, :], windows[blk, "tr"][:].indirect(joints[d][:]), spread[:, d - FIRST_DIRECT, :], MULT
-            )
-
-        pair = keep.tile([P, U], F32, name="pair")
-        nc.vector.tensor_tensor(pair[:], direct[:, 0, :], direct[:, 1, :], ADD)
-        for blk, extra in ((0, direct[:, 2, :]), (1, pair[:])):
+        late = keep.tile([P, len(LATE_TERMS), U], F32, name="late", tag="joint1", align_bytes=MX_ALIGN)
+        for i, (blk, d) in enumerate(LATE_TERMS):
+            looked_up = windows[blk, "tr"][:].indirect(joints[d][:])
+            nc.vector.tensor_tensor(late[:, i, :], looked_up, late_weights[:, d - FIRST_LATE_JOINT, :], MULT)
+        late_pair = keep.tile([P, U], F32, name="late_pair")
+        nc.vector.tensor_tensor(late_pair[:], late[:, 0, :], late[:, 1, :], ADD)
+        for blk, late_sum in enumerate((late[:, 2, :], late_pair[:])):
             result = keep.tile([P, U], F32, name=f"result{blk}")
-            nc.vector.tensor_tensor(result[:], totals[blk][:], extra, ADD)
+            nc.vector.tensor_tensor(result[:], totals[blk][:].rearrange("p h r -> p (h r)"), late_sum, ADD)
             nc.sync.dma_start(out[blk * P : (blk + 1) * P, :], result[:])

@@ -201,8 +201,35 @@ def tile_picked_yskinlb_lin_p_kernel(
         look_up(0, [("rb", d) for d in range(D)], "stage3")
         make_window((1, "rb"))
         look_up(1, [("tr", d) for d in range(D)], "stage4")
-        for d in range(D):
+        for d in range(D - 1):
             look_up(1, [("ra", d), ("rb", d)], f"joint{d}")
+        last_terms = keep.tile([P, 2, HALVES, P], F32, name="last_terms")
+        last_weighted = keep.tile([P, HALVES, P], F32, name="last_weighted")
+        nc.vector.tensor_tensor(
+            last_terms[:, 0].rearrange("p h r -> p (h r)"),
+            windows[1, "ra"][:].indirect(joints[D - 1][:]),
+            rest["ra"][:, 1, :],
+            MULT,
+        )
+        for h in range(HALVES):
+            bank = product_bank([P, P])
+            entries = slice(h * P // LIST_ROWS, (h + 1) * P // LIST_ROWS)
+            looked_up = windows[1, "rb"][:].indirect(joints[D - 1][:, entries])
+            nc.vector.tensor_tensor(last_terms[:, 1, h, :], looked_up, rest["rb"][:, 1, h * P : (h + 1) * P], MULT)
+            for i in range(2):
+                nc.tensor.matmul(
+                    bank[:], last_terms[:, i, h, :], identity[:], start=i == 0, stop=i == 1, is_transpose=True
+                )
+            col = HALVES * (D - 1) + h
+            nc.scalar.activation(last_weighted[:, h, :], bank[:], COPY, scale=weight_cols[:, col : col + 1])
+            nc.tensor.matmul(
+                totals[1][:, h, :],
+                last_weighted[:, h, :],
+                identity[:],
+                start=False,
+                stop=h == HALVES - 1,
+                is_transpose=True,
+            )
 
         late = keep.tile([P, len(LATE_TERMS), U], F32, name="late", tag="joint1", align_bytes=MX_ALIGN)
         for i, (blk, d) in enumerate(LATE_TERMS):
@@ -212,5 +239,9 @@ def tile_picked_yskinlb_lin_p_kernel(
         nc.vector.tensor_tensor(late_pair[:], late[:, 0, :], late[:, 1, :], ADD)
         for blk, late_sum in enumerate((late[:, 2, :], late_pair[:])):
             result = keep.tile([P, U], F32, name=f"result{blk}")
-            nc.vector.tensor_tensor(result[:], totals[blk][:].rearrange("p h r -> p (h r)"), late_sum, ADD)
-            nc.sync.dma_start(out[blk * P : (blk + 1) * P, :], result[:])
+            total = totals[blk][:].rearrange("p h r -> p (h r)")
+            width = U // (blk + 1)
+            for lo in range(0, U, width):
+                cols = slice(lo, lo + width)
+                nc.vector.tensor_tensor(result[:, cols], total[:, cols], late_sum[:, cols], ADD)
+                nc.sync.dma_start(out[blk * P : (blk + 1) * P, cols], result[:, cols])

from contextlib import ExitStack

import concourse.mybir as mybir
from concourse.masks import make_identity

K, T, S, N, U, D = 512, 1024, 512, 256, 256, 4
FLOPS = 3 * 2 * K * N * S

F32 = mybir.dt.float32
BF16 = mybir.dt.bfloat16
I32 = mybir.dt.int32
U32 = mybir.dt.uint32
U16 = mybir.dt.uint16
U8 = mybir.dt.uint8
FP8X4 = mybir.dt.float8_e4m3fn_x4
COPY = mybir.ActivationFunctionType.Copy
MULT = mybir.AluOpType.mult
ADD = mybir.AluOpType.add

P = 128
PACK = 4
QUADRANT = 32
LIST_ROWS = 16
LINE = 4
BLOCKS = N // P
HALVES = U // P
MX_ALIGN = 64

HALF = S // 2
PIECES = ((0, 0, HALF), (1, 0, HALF // 2), (1, HALF // 2, HALF))

LATE_TERMS = ((1, 2), (1, 3), (0, 3))
FIRST_LATE_JOINT = min(d for blk, d in LATE_TERMS)


def tile_picked_yskinlb_lin_p_kernel(
    tc, x_words, x_scales, w1, w2, w3, px, py, wgt, offs, jt1, jt2, jt3, jt4, out
):
    nc = tc.nc
    with ExitStack() as ctx:
        keep = ctx.enter_context(tc.tile_pool(name="keep", bufs=1))
        psum = ctx.enter_context(tc.psum_pool(name="psum", bufs=1))

        def product_bank(shape):
            return psum.tile(shape, F32, name="product", bufs=2)

        def joint_bank(shape):
            return psum.tile(shape, F32, name="joint_sum", bufs=D)

        staged = [[(0, "tr")], [(0, "ra")], [(0, "rb")], [(1, "tr"), (1, "ra")], [(1, "rb")]]
        raw = {}
        for i, keys in enumerate(staged):
            stage = keep.tile([P, len(keys), PACK, P], F32, name=f"raw{i}", tag=f"stage{i}", align_bytes=MX_ALIGN)
            for slot, key in enumerate(keys):
                raw[key] = stage[:, slot]
        weights = {"ra": w1, "rb": w2, "tr": w3}

        def load_weight(blk, name):
            rows = weights[name].rearrange("(p t) m -> p t m", t=PACK)
            nc.sync.dma_start(raw[blk, name], rows[:, :, blk * P : (blk + 1) * P])

        def load_list(src, name):
            tile = keep.tile(list(src.shape), U16, name=name)
            nc.sync.dma_start(tile[:], src)
            return tile

        def load_rest(src, name):
            tile = keep.tile([P, BLOCKS, U], F32, name=name)
            nc.sync.dma_start(tile[:], src.rearrange("(b p) r -> p b r", p=P))
            return tile

        scale_table = keep.tile([P, T], U8, name="scale_table", align_bytes=MX_ALIGN)
        nc.gpsimd.memset(scale_table[:].bitcast(I32), 0)
        picks = load_list(offs, "picks")
        load_weight(0, "tr")
        for q in range(P // QUADRANT):
            nc.sync.dma_start(
                scale_table[QUADRANT * q : QUADRANT * q + 4, :].bitcast(I32),
                x_scales[0, 4 * q : 4 * q + 4, :].bitcast(I32),
            )
        word_table = keep.tile([P, T], U32, name="word_table", align_bytes=MX_ALIGN)
        nc.sync.dma_start(word_table[:].bitcast(I32), x_words[0].rearrange("p n t -> p (n t)").bitcast(I32))
        load_weight(0, "ra")
        joints = [load_list(jt1, "joints0")]
        load_weight(0, "rb")
        joints.append(load_list(jt2, "joints1"))
        joints.append(load_list(jt3, "joints2"))
        rest = {"ra": load_rest(px, "rest_x")}
        joints.append(load_list(jt4, "joints3"))
        load_weight(1, "tr")
        weight_rows = keep.tile([P, P], F32, name="weight_rows")
        nc.gpsimd.memset(weight_rows[:], 0.0)
        nc.sync.dma_start(weight_rows[0 : D * HALVES, :], wgt[:, 0, :].rearrange("d (h r) -> d h r", r=P))
        load_weight(1, "ra")
        rest["rb"] = load_rest(py, "rest_y")
        load_weight(1, "rb")
        late_weights = keep.tile([P, D - FIRST_LATE_JOINT, U], F32, name="late_weights")
        nc.sync.dma_start(late_weights[:], wgt[FIRST_LATE_JOINT:D].rearrange("d p r -> p d r"))

        identity = keep.tile([P, P], F32, name="identity")
        make_identity(nc, identity[:])

        windows = {key: keep.tile([P, S], F32, name=f"window_{key[1]}{key[0]}") for key in raw}

        def quantise(key):
            blk, name = key
            grouped = keep.tile([P, P, PACK], BF16, name=f"grouped_{name}{blk}", align_bytes=MX_ALIGN)
            nc.scalar.copy(
                grouped[:].rearrange("p (c i) t -> p c t i", i=LINE),
                raw[key].rearrange("p t (c i) -> p c t i", i=LINE),
            )
            codes = keep.tile([P, P], U32, name=f"codes_{name}{blk}", align_bytes=MX_ALIGN)
            scales = keep.tile([P, P], U8, name=f"scales_{name}{blk}", align_bytes=MX_ALIGN)
            nc.vector.quantize_mx(
                out=codes[:].bitcast(FP8X4), scales=scales[:], in_=grouped[:].rearrange("p c t -> p (c t)")
            )
            return codes, scales

        def multiply(dst, quantised, half, lo, hi):
            codes, scales = quantised
            nc.tensor.matmul_mx(
                out=dst,
                lhsT=codes[:].bitcast(FP8X4),
                lhsT_scale=scales[:],
                rhs=picked_words[half][:, lo:hi].bitcast(FP8X4),
                rhs_scale=picked_scales[:, half * HALF + lo : half * HALF + hi],
                start=True,
                stop=True,
            )

        def make_window(key):
            quantised = quantise(key)
            bank = product_bank([P, S])
            for half in range(2):
                multiply(bank[:, half * HALF : (half + 1) * HALF], quantised, half, 0, HALF)
            nc.scalar.activation(windows[key][:], bank[:], COPY, scale=-1.0 if key[1] == "rb" else 1.0)

        picked_scales = keep.tile([P, S], U8, name="picked_scales", align_bytes=MX_ALIGN)
        nc.vector.tensor_copy(picked_scales[:], scale_table[:].indirect(picks[:]))
        first_weight = quantise((0, "tr"))
        picked_words = [
            keep.tile([P, HALF], U32, name=f"picked_words{half}", tag=tag, align_bytes=MX_ALIGN)
            for half, tag in enumerate(("picked_words", "stage0"))
        ]
        piece_banks = []
        for half, lo, hi in PIECES:
            entries = slice((half * HALF + lo) // LIST_ROWS, (half * HALF + hi) // LIST_ROWS)
            nc.vector.tensor_copy(picked_words[half][:, lo:hi], word_table[:].indirect(picks[:, entries]))
            piece_banks.append(joint_bank([P, hi - lo]))
            multiply(piece_banks[-1][:], first_weight, half, lo, hi)
        for (half, lo, hi), bank in zip(PIECES, piece_banks):
            nc.vector.tensor_copy(windows[0, "tr"][:, half * HALF + lo : half * HALF + hi], bank[:])
        make_window((0, "ra"))

        totals = [psum.tile([P, HALVES, P], F32, name=f"total{blk}") for blk in range(BLOCKS)]
        joint_sums = {}
        weight_cols = keep.tile([P, D * HALVES], F32, name="weight_cols")

        def add_transposed(bank, src, first, last):
            for h in range(HALVES):
                nc.tensor.matmul(
                    bank[:, h, :],
                    src[:, h, :],
                    identity[:],
                    start=first and h == 0,
                    stop=last and h == HALVES - 1,
                    is_transpose=True,
                )

        def look_up(blk, items, tag):
            items = [(name, d) for name, d in items if name != "tr" or (blk, d) not in LATE_TERMS]
            terms = keep.tile([P, len(items), U], F32, name=f"terms_{tag}", tag=tag, align_bytes=MX_ALIGN)
            for i, (name, d) in enumerate(items):
                looked_up = windows[blk, name][:].indirect(joints[d][:])
                if name == "tr":
                    nc.vector.tensor_copy(terms[:, i, :], looked_up)
                else:
                    nc.vector.tensor_tensor(terms[:, i, :], looked_up, rest[name][:, blk, :], MULT)
                opens = (blk, d) not in joint_sums
                if opens:
                    joint_sums[blk, d] = joint_bank([P, HALVES, P])
                halves = terms[:, i, :].rearrange("p (h r) -> p h r", h=HALVES)
                add_transposed(joint_sums[blk, d], halves, opens, name == "rb")
                if name == "rb":
                    weighted = keep.tile([P, HALVES, P], F32, name="weighted", bufs=D)
                    for h in range(HALVES):
                        col = HALVES * d + h
                        nc.scalar.activation(
                            weighted[:, h, :], joint_sums[blk, d][:, h, :], COPY, scale=weight_cols[:, col : col + 1]
                        )
                    add_transposed(totals[blk], weighted, d == 0, d == D - 1)

        look_up(0, [("tr", d) for d in range(D)], "stage1")
        make_window((0, "rb"))
        look_up(0, [("ra", d) for d in range(D)], "stage2")
        make_window((1, "tr"))
        turned_weights = product_bank([P, P])
        nc.tensor.transpose(turned_weights[:], weight_rows[:], identity[:])
        nc.scalar.copy(weight_cols[:], turned_weights[:, 0 : D * HALVES])
        make_window((1, "ra"))
        look_up(0, [("rb", d) for d in range(D)], "stage3")
        make_window((1, "rb"))
        look_up(1, [("tr", d) for d in range(D)], "stage4")
        for d in range(D - 1):
            look_up(1, [("ra", d), ("rb", d)], f"joint{d}")
        last_terms = keep.tile([P, 2, HALVES, P], F32, name="last_terms")
        last_weighted = keep.tile([P, HALVES, P], F32, name="last_weighted")
        nc.vector.tensor_tensor(
            last_terms[:, 0].rearrange("p h r -> p (h r)"),
            windows[1, "ra"][:].indirect(joints[D - 1][:]),
            rest["ra"][:, 1, :],
            MULT,
        )
        for h in range(HALVES):
            bank = product_bank([P, P])
            entries = slice(h * P // LIST_ROWS, (h + 1) * P // LIST_ROWS)
            looked_up = windows[1, "rb"][:].indirect(joints[D - 1][:, entries])
            nc.vector.tensor_tensor(last_terms[:, 1, h, :], looked_up, rest["rb"][:, 1, h * P : (h + 1) * P], MULT)
            for i in range(2):
                nc.tensor.matmul(
                    bank[:], last_terms[:, i, h, :], identity[:], start=i == 0, stop=i == 1, is_transpose=True
                )
            col = HALVES * (D - 1) + h
            nc.scalar.activation(last_weighted[:, h, :], bank[:], COPY, scale=weight_cols[:, col : col + 1])
            nc.tensor.matmul(
                totals[1][:, h, :],
                last_weighted[:, h, :],
                identity[:],
                start=False,
                stop=h == HALVES - 1,
                is_transpose=True,
            )

        late = keep.tile([P, len(LATE_TERMS), U], F32, name="late", tag="joint1", align_bytes=MX_ALIGN)
        for i, (blk, d) in enumerate(LATE_TERMS):
            looked_up = windows[blk, "tr"][:].indirect(joints[d][:])
            nc.vector.tensor_tensor(late[:, i, :], looked_up, late_weights[:, d - FIRST_LATE_JOINT, :], MULT)
        late_pair = keep.tile([P, U], F32, name="late_pair")
        nc.vector.tensor_tensor(late_pair[:], late[:, 0, :], late[:, 1, :], ADD)
        for blk, late_sum in enumerate((late[:, 2, :], late_pair[:])):
            result = keep.tile([P, U], F32, name=f"result{blk}")
            total = totals[blk][:].rearrange("p h r -> p (h r)")
            width = U // (blk + 1)
            for lo in range(0, U, width):
                cols = slice(lo, lo + width)
                nc.vector.tensor_tensor(result[:, cols], total[:, cols], late_sum[:, cols], ADD)
                nc.sync.dma_start(out[blk * P : (blk + 1) * P, cols], result[:, cols])
